import numpy as np
import ml_dtypes


def mxq(x, axis, fmt="e4m3"):
    dtype, down = {"e4m3": (ml_dtypes.float8_e4m3fn, 7), "e5m2": (ml_dtypes.float8_e5m2, 14)}[fmt]
    v = np.moveaxis(np.asarray(x, np.float32).astype(ml_dtypes.bfloat16).astype(np.float64), axis, -1)
    blocks = v.reshape(v.shape[:-1] + (-1, 32))
    amax = np.abs(blocks).max(-1, keepdims=True)
    byte = np.maximum(np.where(amax > 0, np.frexp(amax)[1] - 1 + 127, 0) - down, 1)
    scale = np.exp2(byte - 127.0)
    codes = (blocks / scale).astype(np.float32).astype(dtype).astype(np.float64)
    return np.moveaxis((codes * scale).reshape(v.shape), -1, axis)


WIDE = False


def mx_kscale(k):
    if not WIDE:
        return np.ones(k)
    levels = np.array([10, -10, 5, -5, 0])
    if k % 512:
        return np.exp2(np.random.permutation(np.resize(levels, k // 32))).repeat(32)
    a = np.empty((k // 512, 16))
    for p in range(k // 512):
        a[p, :8] = np.random.permutation(np.resize(levels, 8))
        for g in range(8):
            far = levels[np.abs(levels - a[p, g]) >= 10]
            a[p, g + 8] = far[np.random.randint(len(far))]
    return np.exp2(a.ravel()).repeat(32)


def f64(x):
    return np.asarray(x).astype(np.float64)


def striped(idx):
    return np.tile(idx.reshape(-1, 16).T, (8, 1)).astype(np.uint16)


def unstriped(offs):
    return offs[:16].T.reshape(-1).astype(np.int64)


def striped8(idx):
    return np.concatenate([x.reshape(-1, 16).T for x in idx]).astype(np.uint16)


def runs(offs, k):
    lists = np.stack([offs[16 * r : 16 * r + 16].T.reshape(-1) for r in range(8)]).astype(np.int64)
    return lists[np.arange(k) % 512 // 64]


def pack_weight(w):
    k, n = w.shape
    w = f64(np.asarray(w, np.float32).astype(ml_dtypes.bfloat16)).reshape(k // 32, 32, n)
    amax = np.abs(w).max(1)
    byte = np.clip(np.where(amax > 0, np.frexp(amax)[1] - 1 + 127 - 7, 1), 1, 254)
    scaled = (w * np.exp2(127.0 - byte)[:, None, :]).reshape(k, n).astype(np.float32)
    words = np.ascontiguousarray(scaled.reshape(k // 512, 128, 4, n).transpose(0, 1, 3, 2)).astype(ml_dtypes.float8_e4m3fn).view(np.uint8)
    return words, np.ascontiguousarray(byte.astype(np.uint8).reshape(k // 512, 16, n))


def unpack_weight(words, scales):
    g, p, n, _ = words.shape
    vals = np.ascontiguousarray(words).view(ml_dtypes.float8_e4m3fn).astype(np.float64) * np.repeat(np.exp2(scales.astype(np.float64) - 127.0), 8, axis=1)[..., None]
    return vals.transpose(0, 1, 3, 2).reshape(g * 512, n)


E2M1 = np.array([0.0, 0.5, 1.0, 1.5, 2.0, 3.0, 4.0, 6.0, -0.0, -0.5, -1.0, -1.5, -2.0, -3.0, -4.0, -6.0])


def pack_fp4(w):
    k, n = w.shape
    w = f64(np.asarray(w, np.float32).astype(ml_dtypes.bfloat16)).reshape(k // 32, 32, n)
    amax = np.abs(w).max(1)
    mant, ex = np.frexp(amax / 6.0)
    byte = np.clip(np.where(amax > 0, np.where(mant > 0.5, ex, ex - 1) + 127, 1), 1, 254)
    scaled = (w * np.exp2(127.0 - byte)[:, None, :]).reshape(k, n).astype(np.float32)
    c = np.ascontiguousarray(scaled.reshape(k // 512, 128, 4, n).transpose(0, 1, 3, 2)).astype(ml_dtypes.float4_e2m1fn).view(np.uint8) & 0xF
    words = (c[..., 0::2] | (c[..., 1::2] << 4)).reshape(k // 512, 128, 2 * n)
    return np.ascontiguousarray(words), np.ascontiguousarray(byte.astype(np.uint8).reshape(k // 512, 16, n))


def unpack_fp4(words, scales):
    g, _, n = scales.shape
    words = np.ascontiguousarray(words).reshape(g, 128, n, 2)
    nib = np.empty((g, 128, n, 4), np.uint8)
    nib[..., 0::2] = words & 0xF
    nib[..., 1::2] = words >> 4
    vals = E2M1[nib] * np.repeat(np.exp2(scales.astype(np.float64) - 127.0), 8, axis=1)[..., None]
    return vals.transpose(0, 1, 3, 2).reshape(g * 512, n)


def planes(y):
    n, m = y.shape
    v = y.astype(np.float32).astype(ml_dtypes.bfloat16).astype(np.float64).reshape(n // 32, 32, m)
    top = np.abs(v).max(1)
    byte = np.clip(np.where(top > 0, np.frexp(top)[1] - 1 + 127 - 7, 1), 1, 254)
    codes = (v * np.exp2(127.0 - byte)[:, None, :]).reshape(n, m).astype(np.float32).astype(ml_dtypes.float8_e4m3fn).view(np.uint8)
    words = codes.reshape(n // 512, 128, 4, m).transpose(0, 1, 3, 2)
    return np.ascontiguousarray(words), np.ascontiguousarray(byte.astype(np.uint8).reshape(n // 512, 16, m))


K, T, S, V, N, H = 512, 2048, 512, 256, 512, 512


def setup_inputs():
    n = np.random.standard_normal
    s = mx_kscale(K)[:, None]
    u = mx_kscale(H)
    packed_xT = pack_weight(n((K, T)) * s)
    packed_w1 = pack_fp4(n((K, H)) / np.sqrt(K) / s)
    packed_w2 = pack_fp4(n((H, N)) / np.sqrt(H) / u[:, None])
    perm = np.stack([np.random.permutation(S) for _ in range(8)])
    perm2 = np.stack([np.random.permutation(S) for _ in range(8)])
    return {
        "x_words": packed_xT[0],
        "x_scales": packed_xT[1],
        "w1_words": packed_w1[0],
        "w1_scales": packed_w1[1],
        "gn": (np.random.uniform(0.5, 1.5, (H, 1)) * u[:, None]).astype(np.float32),
        "w2_words": packed_w2[0],
        "w2_scales": packed_w2[1],
        "offs": striped(np.random.permutation(T)[:S]),
        "la": striped8(perm[:, :V]),
        "lb": striped8(perm[:, V:]),
        "ma": striped8(perm2[:, :V]),
        "mb": striped8(perm2[:, V:]),
    }


def reference(x_words, x_scales, w1_words, w1_scales, gn, w2_words, w2_scales, offs, la, lb, ma, mb):
    xq = unpack_weight(x_words, x_scales)[:, unstriped(offs)]
    y = unpack_fp4(w1_words, w1_scales).T @ xq
    b = y[np.arange(H)[:, None], runs(lb, H)]
    a = y[np.arange(H)[:, None], runs(la, H)]
    c1 = 0.75 * ((a - b) / (np.abs(a - b) + 1))
    b1 = b + c1
    a1 = a - c1
    h0 = np.zeros((H, S))
    h0[np.arange(H)[:, None], runs(la, H)] = a1
    h = h0.copy()
    h[np.arange(H)[:, None], runs(lb, H)] = b1
    qv = h[np.arange(H)[:, None], runs(mb, H)]
    p = h[np.arange(H)[:, None], runs(ma, H)]
    c2 = 0.75 * ((p - qv) / (np.abs(p - qv) + 1))
    q1 = qv + c2
    p1 = p - c2
    h2 = np.zeros((H, S))
    h2[np.arange(H)[:, None], runs(ma, H)] = p1
    h3 = h2.copy()
    h3[np.arange(H)[:, None], runs(mb, H)] = q1
    z = f64(gn) * h3
    out_0 = unpack_fp4(w2_words, w2_scales).T @ mxq(z, 0, "e4m3")
    return (out_0,) + planes(out_0)

@@ -1,0 +1,197 @@
+import math
+from contextlib import ExitStack
+
+import concourse.mybir as mybir
+
+K, T, S, V, N, H = 512, 2048, 512, 256, 512, 512
+FLOPS = 2 * K * H * S + 2 * H * N * S
+
+F32 = mybir.dt.float32
+BF16 = mybir.dt.bfloat16
+I32 = mybir.dt.int32
+U32 = mybir.dt.uint32
+U16 = mybir.dt.uint16
+U8 = mybir.dt.uint8
+FP8X4 = mybir.dt.float8_e4m3fn_x4
+FP4X4 = mybir.dt.float4_e2m1fn_x4
+ACT = mybir.ActivationFunctionType
+ALU = mybir.AluOpType
+
+P = 128
+PACK = 4
+HALF = S // 2
+CH = 128
+
+
+def tile_picked_pbd2_none_po_kernel(
+    tc, x_words, x_scales, w1_words, w1_scales, gn, w2_words, w2_scales, offs, la, lb, ma, mb, out_0, out_1, out_2
+):
+    nc = tc.nc
+    with ExitStack() as ctx:
+        lists = ctx.enter_context(tc.tile_pool(name="lists", bufs=1))
+        sb = ctx.enter_context(tc.tile_pool(name="sb", bufs=1))
+        psum = ctx.enter_context(tc.psum_pool(name="psum", bufs=8))
+
+        def load_list(src, name):
+            tile = lists.tile(list(src.shape), U16, name=name)
+            nc.sync.dma_start(tile[:], src)
+            return tile
+
+        def load_scale_rows(queues, tile, src):
+            for q in range(4):
+                queues[q].dma_start(tile[32 * q : 32 * q + 4, :].bitcast(I32), src[0, 4 * q : 4 * q + 4, :].bitcast(I32))
+
+        xs = sb.tile([P, T], U8, name="xs", align_bytes=64)
+        w1s_raw = sb.tile([P, H], U8, name="w1s_raw", align_bytes=64)
+        w1w_raw = sb.tile([P, 2 * H], U8, name="w1w_raw", align_bytes=64)
+        xw = sb.tile([P, T], U32, name="xw", align_bytes=64)
+        nc.vector.memset(xs[:].bitcast(I32), 0)
+        nc.gpsimd.memset(w1s_raw[:].bitcast(I32), 0)
+        offs_t = load_list(offs, "offs_t")
+        nc.sync.dma_start(w1w_raw[:].bitcast(I32), w1_words[0].bitcast(I32))
+        la_t = load_list(la, "la_t")
+        nc.sync.dma_start(xw[:].bitcast(I32), x_words[0].rearrange("p n t -> p (n t)").bitcast(I32))
+        load_scale_rows([nc.sync] * 4, xs, x_scales)
+        load_scale_rows([nc.sync, nc.sync, nc.gpsimd, nc.gpsimd], w1s_raw, w1_scales)
+        lb_t = load_list(lb, "lb_t")
+        ma_t = load_list(ma, "ma_t")
+        mb_t = load_list(mb, "mb_t")
+
+        def deal(words_raw, scales_raw, name):
+            words = sb.tile([P, 2 * H], U8, name=name + "w", align_bytes=64)
+            scales = sb.tile([P, H], U8, name=name + "s", align_bytes=64)
+            nc.scalar.copy(
+                words[:].bitcast(U16).rearrange("p (t m) -> p t m", t=PACK),
+                words_raw[:].bitcast(U16).rearrange("p (m t) -> p t m", t=PACK),
+            )
+            nc.vector.tensor_copy(
+                scales[:].rearrange("p (t m) -> p t m", t=PACK),
+                scales_raw[:].rearrange("p (m t) -> p t m", t=PACK),
+            )
+            return words, scales
+
+        xqs = sb.tile([P, S], U8, name="xqs", align_bytes=64)
+        nc.vector.tensor_copy(xqs[:], xs[:].indirect(offs_t[:]))
+        w1w, w1s = deal(w1w_raw, w1s_raw, "w1")
+        nc.sync.dma_start(w1w_raw[:].bitcast(I32), w2_words[0].bitcast(I32))
+        load_scale_rows([nc.sync] * 4, w1s_raw, w2_scales)
+        xq = []
+        for hf in range(2):
+            words = sb.tile([P, HALF], U32, name=f"xq{hf}", align_bytes=64)
+            nc.vector.tensor_copy(words[:], xw[:].indirect(offs_t[:, hf * HALF // 16 : (hf + 1) * HALF // 16]))
+            xq.append(words)
+
+        size = [sb.tile([P, V], F32, name=f"size{u}", tag=f"size{u}", align_bytes=64) for u in range(2 * PACK)]
+        y = {}
+
+        def project(t):
+            y[t] = sb.tile([P, S], F32, name=f"y{t}", tag=f"size{t - 2}" if t >= 2 else f"y{t}", align_bytes=64)
+            for hf in range(2):
+                cols = slice(hf * HALF, (hf + 1) * HALF)
+                bank = psum.tile([P, HALF], F32, name="bank")
+                nc.tensor.matmul_mx(
+                    bank[:],
+                    lhsT=w1w[:, 2 * P * t : 2 * P * (t + 1)].bitcast(FP4X4),
+                    lhsT_scale=w1s[:, P * t : P * (t + 1)],
+                    rhs=xq[hf][:].bitcast(FP8X4),
+                    rhs_scale=xqs[:, cols],
+                    start=True,
+                    stop=True,
+                )
+                if t == 0 and hf == 1:
+                    nc.vector.tensor_copy(y[t][:, cols], bank[:])
+                else:
+                    nc.scalar.copy(y[t][:, cols], bank[:])
+
+        h = [sb.tile([P, S], F32, name=f"h{t}") for t in range(PACK)]
+        h3 = [sb.tile([P, S], F32, name=f"h3{t}") for t in range(PACK)]
+        units = [(y, h, la_t, lb_t)] * PACK + [(h, h3, ma_t, mb_t)] * PACK
+        last = len(units) - 1
+        a = [sb.tile([P, V], F32, name=f"a{u}") for u in range(len(units))]
+        b = [sb.tile([P, V], F32, name=f"b{u}") for u in range(len(units))]
+        d = [sb.tile([P, V], F32, name=f"d{u}") for u in range(len(units))]
+        r = [sb.tile([P, V], F32, name=f"r{u}") for u in range(len(units))]
+
+        def fetch(u):
+            src, dst, first, second = units[u]
+            if u < PACK:
+                project(u)
+            window = src[u % PACK]
+            if u < 2:
+                nc.vector.tensor_copy(b[u][:], window[:].indirect(second[:]))
+                nc.vector.tensor_tensor(d[u][:], window[:].indirect(first[:]), b[u][:], ALU.subtract)
+                nc.scalar.activation(a[u][:], window[:].indirect(first[:]), ACT.Copy)
+            else:
+                nc.scalar.activation(a[u][:], window[:].indirect(first[:]), ACT.Copy)
+                nc.scalar.activation(b[u][:], window[:].indirect(second[:]), ACT.Copy)
+                nc.vector.tensor_tensor(d[u][:], a[u][:], b[u][:], ALU.subtract)
+
+        def weigh(u):
+            nc.scalar.activation(size[u][:], d[u][:], ACT.Abs)
+            nc.scalar.activation(r[u][:], size[u][:], ACT.Abs_reciprocal_sqrt, bias=1.0)
+            nc.scalar.activation(r[u][:], r[u][:], ACT.Square, scale=math.sqrt(0.75))
+
+        def correct(u):
+            nc.vector.tensor_tensor(r[u][:], d[u][:], r[u][:], ALU.mult)
+            nc.scalar.activation(d[u][:], r[u][:], ACT.Copy, scale=-1.0)
+
+        def put_back(u):
+            src, dst, first, second = units[u]
+            nc.vector.tensor_tensor(dst[u % PACK][:].indirect(second[:]), b[u][:], r[u][:], ALU.add)
+            nc.vector.tensor_tensor(dst[u % PACK][:].indirect(first[:]), a[u][:], d[u][:], ALU.add)
+
+        fetch(0)
+        weigh(0)
+        fetch(1)
+        for u in range(len(units)):
+            correct(u)
+            if u < last:
+                weigh(u + 1)
+            if u + 2 <= last:
+                fetch(u + 2)
+            put_back(u)
+
+
+        w2w, w2s = deal(w1w_raw, w1s_raw, "w1")
+        gain = sb.tile([P, PACK], F32, name="gain", tag="xqs", align_bytes=64)
+        nc.sync.dma_start(gain[:], gn.rearrange("(p t) o -> p (t o)", t=PACK))
+        z = sb.tile([P, S, PACK], BF16, name="z", tag=f"size{last}", align_bytes=64)
+        for t in range(PACK - 1):
+            nc.scalar.activation(z[:, :, t], h3[t][:], ACT.Copy, scale=gain[:, t : t + 1])
+        ow = sb.tile([P, S], U32, name="ow", align_bytes=64)
+        osc = sb.tile([P, S], U8, name="osc", align_bytes=64)
+        out_rows = out_0.rearrange("(p t) n -> p t n", t=PACK)
+        out_words = out_1[0].rearrange("p n t -> p (n t)").bitcast(I32)
+        for ch in range(S // CH):
+            cols = slice(ch * CH, (ch + 1) * CH)
+            nc.scalar.activation(z[:, cols, PACK - 1], h3[PACK - 1][:, cols], ACT.Copy, scale=gain[:, PACK - 1 : PACK])
+        for ch in range(S // CH):
+            cols = slice(ch * CH, (ch + 1) * CH)
+            zw = sb.tile([P, CH], U32, name=f"zw{ch}", align_bytes=64)
+            zs = sb.tile([P, CH], U8, name=f"zs{ch}", align_bytes=64)
+            nc.vector.quantize_mx(zw[:].bitcast(FP8X4), zs[:], z[:, cols, :].rearrange("p c t -> p (c t)"))
+            res = sb.tile([P, PACK, CH], F32, name=f"res{ch}")
+            for pair in range(2):
+                bank = psum.tile([P, 2, CH], F32, name="bank")
+                for j in range(2):
+                    t = 2 * pair + j
+                    nc.tensor.matmul_mx(
+                        bank[:, j, :],
+                        lhsT=w2w[:, 2 * P * t : 2 * P * (t + 1)].bitcast(FP4X4),
+                        lhsT_scale=w2s[:, P * t : P * (t + 1)],
+                        rhs=zw[:].bitcast(FP8X4),
+                        rhs_scale=zs[:],
+                        start=True,
+                        stop=True,
+                    )
+                nc.scalar.copy(res[:, 2 * pair : 2 * pair + 2, :], bank[:])
+            nc.sync.dma_start(out_rows[:, :, cols], res[:])
+            rb = sb.tile([P, CH, PACK], BF16, name=f"rb{ch}", align_bytes=64)
+            nc.vector.tensor_copy(
+                rb[:].rearrange("p (c i) t -> p c t i", i=4), res[:].rearrange("p t (c i) -> p c t i", i=4)
+            )
+            nc.vector.quantize_mx(ow[:, cols].bitcast(FP8X4), osc[:, cols], rb[:].rearrange("p c t -> p (c t)"))
+            nc.sync.dma_start(out_words[:, cols], ow[:, cols].bitcast(I32))
+        for q in range(4):
+            queue = nc.sync if q % 2 else nc.scalar
+            queue.dma_start(out_2[0, 4 * q : 4 * q + 4, :].bitcast(I32), osc[32 * q : 32 * q + 4, :].bitcast(I32))

@@ -109,7 +109,7 @@ def tile_picked_pbd2_none_po_kernel(
         last = len(units) - 1
         a = [sb.tile([P, V], F32, name=f"a{u}") for u in range(len(units))]
         b = [sb.tile([P, V], F32, name=f"b{u}") for u in range(len(units))]
-        d = [sb.tile([P, V], F32, name=f"d{u}") for u in range(len(units))]
+        d = [sb.tile([P, V], F32, name=f"d{u}", tag=f"d{u}") for u in range(len(units))]
         r = [sb.tile([P, V], F32, name=f"r{u}") for u in range(len(units))]
 
         def fetch(u):
@@ -124,7 +124,7 @@ def tile_picked_pbd2_none_po_kernel(
             else:
                 nc.scalar.activation(a[u][:], window[:].indirect(first[:]), ACT.Copy)
                 nc.scalar.activation(b[u][:], window[:].indirect(second[:]), ACT.Copy)
-                nc.vector.tensor_tensor(d[u][:], a[u][:], b[u][:], ALU.subtract)
+                nc.gpsimd.tensor_tensor(d[u][:], a[u][:], b[u][:], ALU.subtract)
 
         def weigh(u):
             nc.scalar.activation(size[u][:], d[u][:], ACT.Abs)
@@ -132,24 +132,34 @@ def tile_picked_pbd2_none_po_kernel(
             nc.scalar.activation(r[u][:], r[u][:], ACT.Square, scale=math.sqrt(0.75))
 
         def correct(u):
-            nc.vector.tensor_tensor(r[u][:], d[u][:], r[u][:], ALU.mult)
-            nc.scalar.activation(d[u][:], r[u][:], ACT.Copy, scale=-1.0)
+            engine = nc.vector if u == 0 else nc.gpsimd
+            engine.tensor_tensor(r[u][:], d[u][:], r[u][:], ALU.mult)
 
-        def put_back(u):
+        def put_second(u):
             src, dst, first, second = units[u]
-            nc.vector.tensor_tensor(dst[u % PACK][:].indirect(second[:]), b[u][:], r[u][:], ALU.add)
-            nc.vector.tensor_tensor(dst[u % PACK][:].indirect(first[:]), a[u][:], d[u][:], ALU.add)
+            engine = nc.vector if u == 0 else nc.gpsimd
+            engine.tensor_tensor(b[u][:], b[u][:], r[u][:], ALU.add)
+            nc.vector.tensor_copy(dst[u % PACK][:].indirect(second[:]), b[u][:])
+
+        def put_first(u):
+            src, dst, first, second = units[u]
+            moved = sb.tile([P, V], F32, name=f"moved{u}", tag=f"d{u + 1}" if u % 2 == 0 else f"moved{u}")
+            nc.gpsimd.tensor_tensor(moved[:], a[u][:], r[u][:], ALU.subtract)
+            nc.vector.tensor_copy(dst[u % PACK][:].indirect(first[:]), moved[:])
 
         fetch(0)
         weigh(0)
         fetch(1)
-        for u in range(len(units)):
-            correct(u)
-            if u < last:
-                weigh(u + 1)
-            if u + 2 <= last:
-                fetch(u + 2)
-            put_back(u)
+        weigh(1)
+        for u in range(0, len(units), 2):
+            for v in (u, u + 1):
+                correct(v)
+                put_second(v)
+            for v in (u, u + 1):
+                if v + 2 <= last:
+                    fetch(v + 2)
+                    weigh(v + 2)
+                put_first(v)
 
 
         w2w, w2s = deal(w1w_raw, w1s_raw, "w1")

@@ -57,14 +57,14 @@ def tile_picked_pbd2_none_po_kernel(
         ma_t = load_list(ma, "ma_t")
         mb_t = load_list(mb, "mb_t")
 
-        def deal(words_raw, scales_raw, name):
-            words = sb.tile([P, 2 * H], U8, name=name + "w", align_bytes=64)
-            scales = sb.tile([P, H], U8, name=name + "s", align_bytes=64)
+        def deal(words_raw, scales_raw, name, engine, words_tag, scales_tag):
+            words = sb.tile([P, 2 * H], U8, name=name + "w", tag=words_tag, align_bytes=64)
+            scales = sb.tile([P, H], U8, name=name + "s", tag=scales_tag, align_bytes=64)
             nc.scalar.copy(
                 words[:].bitcast(U16).rearrange("p (t m) -> p t m", t=PACK),
                 words_raw[:].bitcast(U16).rearrange("p (m t) -> p t m", t=PACK),
             )
-            nc.vector.tensor_copy(
+            engine.tensor_copy(
                 scales[:].rearrange("p (t m) -> p t m", t=PACK),
                 scales_raw[:].rearrange("p (m t) -> p t m", t=PACK),
             )
@@ -72,7 +72,7 @@ def tile_picked_pbd2_none_po_kernel(
 
         xqs = sb.tile([P, S], U8, name="xqs", align_bytes=64)
         nc.vector.tensor_copy(xqs[:], xs[:].indirect(offs_t[:]))
-        w1w, w1s = deal(w1w_raw, w1s_raw, "w1")
+        w1w, w1s = deal(w1w_raw, w1s_raw, "w1", nc.vector, "w1w", "w1s")
         nc.sync.dma_start(w1w_raw[:].bitcast(I32), w2_words[0].bitcast(I32))
         load_scale_rows([nc.sync] * 4, w1s_raw, w2_scales)
         xq = []
@@ -85,7 +85,7 @@ def tile_picked_pbd2_none_po_kernel(
         y = {}
 
         def project(t):
-            y[t] = sb.tile([P, S], F32, name=f"y{t}", tag=f"size{t - 2}" if t >= 2 else f"y{t}", align_bytes=64)
+            y[t] = sb.tile([P, S], F32, name=f"y{t}", tag="size1" if t == 3 else f"y{t}", align_bytes=64)
             for hf in range(2):
                 cols = slice(hf * HALF, (hf + 1) * HALF)
                 bank = psum.tile([P, HALF], F32, name="bank")
@@ -107,44 +107,51 @@ def tile_picked_pbd2_none_po_kernel(
         h3 = [sb.tile([P, S], F32, name=f"h3{t}") for t in range(PACK)]
         units = [(y, h, la_t, lb_t)] * PACK + [(h, h3, ma_t, mb_t)] * PACK
         last = len(units) - 1
-        a = [sb.tile([P, V], F32, name=f"a{u}") for u in range(len(units))]
-        b = [sb.tile([P, V], F32, name=f"b{u}") for u in range(len(units))]
+        root = [sb.tile([P, V], F32, name=f"root{u}", tag=f"root{u}", align_bytes=64) for u in range(len(units))]
+        a, b, c = {}, {}, {}
         d = [sb.tile([P, V], F32, name=f"d{u}", tag=f"d{u}") for u in range(len(units))]
-        r = [sb.tile([P, V], F32, name=f"r{u}") for u in range(len(units))]
+        r = [sb.tile([P, V], F32, name=f"r{u}", tag=f"r{u}", align_bytes=64) for u in range(len(units))]
 
         def fetch(u):
             src, dst, first, second = units[u]
             if u < PACK:
                 project(u)
             window = src[u % PACK]
-            if u < 2:
-                nc.vector.tensor_copy(b[u][:], window[:].indirect(second[:]))
-                nc.vector.tensor_tensor(d[u][:], window[:].indirect(first[:]), b[u][:], ALU.subtract)
-                nc.scalar.activation(a[u][:], window[:].indirect(first[:]), ACT.Copy)
+            pair = sb.tile([P, 2, V], F32, name=f"pair{u}", tag="root1" if u == 2 else f"pair{u}", align_bytes=64)
+            a[u], b[u] = pair[:, 0, :], pair[:, 1, :]
+            if u == 0:
+                nc.scalar.activation(a[u], window[:].indirect(first[:]), ACT.Copy)
+                nc.vector.tensor_copy(b[u], window[:].indirect(second[:]))
+                nc.vector.tensor_tensor(d[u][:], a[u], b[u], ALU.subtract)
+            elif u == 1:
+                nc.vector.tensor_copy(b[u], window[:].indirect(second[:]))
+                nc.vector.tensor_tensor(d[u][:], window[:].indirect(first[:]), b[u], ALU.subtract)
+                nc.gpsimd.tensor_tensor(a[u], d[u][:], b[u], ALU.add)
             else:
-                nc.scalar.activation(a[u][:], window[:].indirect(first[:]), ACT.Copy)
-                nc.scalar.activation(b[u][:], window[:].indirect(second[:]), ACT.Copy)
-                nc.gpsimd.tensor_tensor(d[u][:], a[u][:], b[u][:], ALU.subtract)
+                nc.scalar.activation(a[u], window[:].indirect(first[:]), ACT.Copy)
+                nc.scalar.activation(b[u], window[:].indirect(second[:]), ACT.Copy)
+                nc.gpsimd.tensor_tensor(d[u][:], a[u], b[u], ALU.subtract)
 
         def weigh(u):
             nc.scalar.activation(size[u][:], d[u][:], ACT.Abs)
-            nc.scalar.activation(r[u][:], size[u][:], ACT.Abs_reciprocal_sqrt, bias=1.0)
-            nc.scalar.activation(r[u][:], r[u][:], ACT.Square, scale=math.sqrt(0.75))
+            nc.scalar.activation(root[u][:], size[u][:], ACT.Abs_reciprocal_sqrt, bias=1.0)
+            nc.scalar.activation(r[u][:], root[u][:], ACT.Square, scale=math.sqrt(0.75))
 
         def correct(u):
             engine = nc.vector if u == 0 else nc.gpsimd
-            engine.tensor_tensor(r[u][:], d[u][:], r[u][:], ALU.mult)
+            c[u] = sb.tile([P, V], F32, name=f"c{u}", tag="y1" if u == 0 else f"c{u}", align_bytes=64)
+            engine.tensor_tensor(c[u][:], d[u][:], r[u][:], ALU.mult)
 
         def put_second(u):
             src, dst, first, second = units[u]
             engine = nc.vector if u == 0 else nc.gpsimd
-            engine.tensor_tensor(b[u][:], b[u][:], r[u][:], ALU.add)
-            nc.vector.tensor_copy(dst[u % PACK][:].indirect(second[:]), b[u][:])
+            engine.tensor_tensor(b[u], b[u], c[u][:], ALU.add)
+            nc.vector.tensor_copy(dst[u % PACK][:].indirect(second[:]), b[u])
 
         def put_first(u):
             src, dst, first, second = units[u]
             moved = sb.tile([P, V], F32, name=f"moved{u}", tag=f"d{u + 1}" if u % 2 == 0 else f"moved{u}")
-            nc.gpsimd.tensor_tensor(moved[:], a[u][:], r[u][:], ALU.subtract)
+            nc.gpsimd.tensor_tensor(moved[:], a[u], c[u][:], ALU.subtract)
             nc.vector.tensor_copy(dst[u % PACK][:].indirect(first[:]), moved[:])
 
         fetch(0)
@@ -162,10 +169,10 @@ def tile_picked_pbd2_none_po_kernel(
                 put_first(v)
 
 
-        w2w, w2s = deal(w1w_raw, w1s_raw, "w1")
+        w2w, w2s = deal(w1w_raw, w1s_raw, "w2", nc.gpsimd, "root5", f"c{last}")
         gain = sb.tile([P, PACK], F32, name="gain", tag="xqs", align_bytes=64)
         nc.sync.dma_start(gain[:], gn.rearrange("(p t) o -> p (t o)", t=PACK))
-        z = sb.tile([P, S, PACK], BF16, name="z", tag=f"size{last}", align_bytes=64)
+        z = sb.tile([P, S, PACK], BF16, name="z", tag=f"root{last}", align_bytes=64)
         for t in range(PACK - 1):
             nc.scalar.activation(z[:, :, t], h3[t][:], ACT.Copy, scale=gain[:, t : t + 1])
         ow = sb.tile([P, S], U32, name="ow", align_bytes=64)
@@ -194,7 +201,10 @@ def tile_picked_pbd2_none_po_kernel(
                         start=True,
                         stop=True,
                     )
-                nc.scalar.copy(res[:, 2 * pair : 2 * pair + 2, :], bank[:])
+                if ch == 0:
+                    nc.vector.tensor_copy(res[:, 2 * pair : 2 * pair + 2, :], bank[:])
+                else:
+                    nc.scalar.copy(res[:, 2 * pair : 2 * pair + 2, :], bank[:])
             nc.sync.dma_start(out_rows[:, :, cols], res[:])
             rb = sb.tile([P, CH, PACK], BF16, name=f"rb{ch}", align_bytes=64)
             nc.vector.tensor_copy(

@@ -19,8 +19,15 @@ ALU = mybir.AluOpType
 
 P = 128
 PACK = 4
+QUADRANTS = 4
+BANKS = 8
 HALF = S // 2
-CH = 128
+CHUNK = 128
+LINE = 4
+UNITS = 2 * PACK
+LAST = UNITS - 1
+SCRATCH_BYTES = V * 4
+PAIR_BYTES = 2 * SCRATCH_BYTES
 
 
 def tile_picked_pbd2_none_po_kernel(
@@ -30,7 +37,8 @@ def tile_picked_pbd2_none_po_kernel(
     with ExitStack() as ctx:
         lists = ctx.enter_context(tc.tile_pool(name="lists", bufs=1))
         sb = ctx.enter_context(tc.tile_pool(name="sb", bufs=1))
-        psum = ctx.enter_context(tc.psum_pool(name="psum", bufs=8))
+        placed = ctx.enter_context(tc.tile_pool(name="placed", bufs=1))
+        psum = ctx.enter_context(tc.psum_pool(name="psum", bufs=BANKS))
 
         def load_list(src, name):
             tile = lists.tile(list(src.shape), U16, name=name)
@@ -38,180 +46,214 @@ def tile_picked_pbd2_none_po_kernel(
             return tile
 
         def load_scale_rows(queues, tile, src):
-            for q in range(4):
-                queues[q].dma_start(tile[32 * q : 32 * q + 4, :].bitcast(I32), src[0, 4 * q : 4 * q + 4, :].bitcast(I32))
+            for q in range(QUADRANTS):
+                queues[q].dma_start(
+                    tile[32 * q : 32 * q + 4, :].bitcast(I32), src[0, 4 * q : 4 * q + 4, :].bitcast(I32)
+                )
 
-        xs = sb.tile([P, T], U8, name="xs", align_bytes=64)
-        w1s_raw = sb.tile([P, H], U8, name="w1s_raw", align_bytes=64)
-        w1w_raw = sb.tile([P, 2 * H], U8, name="w1w_raw", align_bytes=64)
-        xw = sb.tile([P, T], U32, name="xw", align_bytes=64)
-        nc.vector.memset(xs[:].bitcast(I32), 0)
-        nc.gpsimd.memset(w1s_raw[:].bitcast(I32), 0)
+        x_scale_table = sb.tile([P, T], U8, name="x_scale_table", align_bytes=64)
+        w_scales_raw = sb.tile([P, H], U8, name="w_scales_raw", align_bytes=64)
+        w_words_raw = sb.tile([P, 2 * H], U8, name="w_words_raw", align_bytes=64)
+        x_word_table = sb.tile([P, T], U32, name="x_word_table", align_bytes=64)
+        nc.vector.memset(x_scale_table[:].bitcast(I32), 0)
+        nc.gpsimd.memset(w_scales_raw[:].bitcast(I32), 0)
         offs_t = load_list(offs, "offs_t")
-        nc.sync.dma_start(w1w_raw[:].bitcast(I32), w1_words[0].bitcast(I32))
+        nc.sync.dma_start(w_words_raw[:].bitcast(I32), w1_words[0].bitcast(I32))
         la_t = load_list(la, "la_t")
-        nc.sync.dma_start(xw[:].bitcast(I32), x_words[0].rearrange("p n t -> p (n t)").bitcast(I32))
-        load_scale_rows([nc.sync] * 4, xs, x_scales)
-        load_scale_rows([nc.sync, nc.sync, nc.gpsimd, nc.gpsimd], w1s_raw, w1_scales)
+        nc.sync.dma_start(x_word_table[:].bitcast(I32), x_words[0].rearrange("p n t -> p (n t)").bitcast(I32))
+        load_scale_rows([nc.sync] * QUADRANTS, x_scale_table, x_scales)
+        load_scale_rows([nc.sync, nc.sync, nc.gpsimd, nc.gpsimd], w_scales_raw, w1_scales)
         lb_t = load_list(lb, "lb_t")
         ma_t = load_list(ma, "ma_t")
         mb_t = load_list(mb, "mb_t")
 
-        def deal(words_raw, scales_raw, name, engine, words_tag, scales_tag):
-            words = sb.tile([P, 2 * H], U8, name=name + "w", tag=words_tag, align_bytes=64)
-            scales = sb.tile([P, H], U8, name=name + "s", tag=scales_tag, align_bytes=64)
+        warm = sb.tile([P, 2], F32, name="warm")
+        nc.vector.memset(warm[:, 0:1], 1.0)
+        nc.scalar.activation(warm[:, 1:2], warm[:, 0:1], ACT.Abs_reciprocal_sqrt, bias=1.0)
+
+        def deal(name, words_tag):
+            words = sb.tile([P, 2 * H], U8, name=name + "_words", tag=words_tag, align_bytes=64)
+            scales = sb.tile([P, H], U8, name=name + "_scales", tag="dealt_scales", align_bytes=64)
             nc.scalar.copy(
                 words[:].bitcast(U16).rearrange("p (t m) -> p t m", t=PACK),
-                words_raw[:].bitcast(U16).rearrange("p (m t) -> p t m", t=PACK),
+                w_words_raw[:].bitcast(U16).rearrange("p (m t) -> p t m", t=PACK),
             )
-            engine.tensor_copy(
+            nc.vector.tensor_copy(
                 scales[:].rearrange("p (t m) -> p t m", t=PACK),
-                scales_raw[:].rearrange("p (m t) -> p t m", t=PACK),
+                w_scales_raw[:].rearrange("p (m t) -> p t m", t=PACK),
             )
             return words, scales
 
-        xqs = sb.tile([P, S], U8, name="xqs", align_bytes=64)
-        nc.vector.tensor_copy(xqs[:], xs[:].indirect(offs_t[:]))
-        w1w, w1s = deal(w1w_raw, w1s_raw, "w1", nc.vector, "w1w", "w1s")
-        nc.sync.dma_start(w1w_raw[:].bitcast(I32), w2_words[0].bitcast(I32))
-        load_scale_rows([nc.sync] * 4, w1s_raw, w2_scales)
-        xq = []
-        for hf in range(2):
-            words = sb.tile([P, HALF], U32, name=f"xq{hf}", align_bytes=64)
-            nc.vector.tensor_copy(words[:], xw[:].indirect(offs_t[:, hf * HALF // 16 : (hf + 1) * HALF // 16]))
-            xq.append(words)
+        def product(bank, words, scales, t, rhs_words, rhs_scales):
+            nc.tensor.matmul_mx(
+                bank,
+                lhsT=words[:, 2 * P * t : 2 * P * (t + 1)].bitcast(FP4X4),
+                lhsT_scale=scales[:, P * t : P * (t + 1)],
+                rhs=rhs_words.bitcast(FP8X4),
+                rhs_scale=rhs_scales,
+                start=True,
+                stop=True,
+            )
 
-        size = [sb.tile([P, V], F32, name=f"size{u}", tag=f"size{u}", align_bytes=64) for u in range(2 * PACK)]
-        y = {}
+        picked_scales = sb.tile([P, S], U8, name="picked_scales", align_bytes=64)
+        nc.vector.tensor_copy(picked_scales[:], x_scale_table[:].indirect(offs_t[:]))
+        w1w, w1s = deal("w1", "w1_words")
+        nc.sync.dma_start(w_words_raw[:].bitcast(I32), w2_words[0].bitcast(I32))
+        load_scale_rows([nc.sync] * QUADRANTS, w_scales_raw, w2_scales)
+        picked_words = []
+        for half in range(2):
+            words = sb.tile([P, HALF], U32, name=f"picked_words{half}", align_bytes=64)
+            entries = offs_t[:, half * HALF // 16 : (half + 1) * HALF // 16]
+            nc.vector.tensor_copy(words[:], x_word_table[:].indirect(entries))
+            picked_words.append(words)
+
+        y = [sb.tile([P, S], F32, name=f"y{t}") for t in range(PACK)]
 
         def project(t):
-            y[t] = sb.tile([P, S], F32, name=f"y{t}", tag="size1" if t == 3 else f"y{t}", align_bytes=64)
-            for hf in range(2):
-                cols = slice(hf * HALF, (hf + 1) * HALF)
+            for half in range(2):
+                cols = slice(half * HALF, (half + 1) * HALF)
                 bank = psum.tile([P, HALF], F32, name="bank")
-                nc.tensor.matmul_mx(
-                    bank[:],
-                    lhsT=w1w[:, 2 * P * t : 2 * P * (t + 1)].bitcast(FP4X4),
-                    lhsT_scale=w1s[:, P * t : P * (t + 1)],
-                    rhs=xq[hf][:].bitcast(FP8X4),
-                    rhs_scale=xqs[:, cols],
-                    start=True,
-                    stop=True,
-                )
-                if t == 0 and hf == 1:
+                product(bank[:], w1w, w1s, t, picked_words[half][:], picked_scales[:, cols])
+                if t == 0 and half == 1:
                     nc.vector.tensor_copy(y[t][:, cols], bank[:])
                 else:
                     nc.scalar.copy(y[t][:, cols], bank[:])
 
         h = [sb.tile([P, S], F32, name=f"h{t}") for t in range(PACK)]
         h3 = [sb.tile([P, S], F32, name=f"h3{t}") for t in range(PACK)]
-        units = [(y, h, la_t, lb_t)] * PACK + [(h, h3, ma_t, mb_t)] * PACK
-        last = len(units) - 1
-        root = [sb.tile([P, V], F32, name=f"root{u}", tag=f"root{u}", align_bytes=64) for u in range(len(units))]
-        a, b, c = {}, {}, {}
-        d = [sb.tile([P, V], F32, name=f"d{u}", tag=f"d{u}") for u in range(len(units))]
-        r = [sb.tile([P, V], F32, name=f"r{u}", tag=f"r{u}", align_bytes=64) for u in range(len(units))]
+        source, target = y + h, h + h3
+        first_list = [la_t] * PACK + [ma_t] * PACK
+        second_list = [lb_t] * PACK + [mb_t] * PACK
+        a, b, d, r, c = {}, {}, {}, {}, {}
+
+        def scratch(name, tag=None):
+            return sb.tile([P, V], F32, name=name, tag=tag or name, align_bytes=64)
+
+        def d_tag(u):
+            if u < PACK:
+                return f"d{u}"
+            return f"r{u - 1}" if u % 2 == 0 else f"c{u - 3}"
+
+        def gather_on_scalar(out, u, entries):
+            nc.scalar.activation(out, source[u][:].indirect(entries[:]), ACT.Copy)
+
+        def fetch_first(u, tag):
+            a[u] = scratch(f"a{u}", tag)[:]
+            gather_on_scalar(a[u], u, first_list[u])
+
+        def fetch_second_on_vector(u):
+            b[u] = scratch(f"b{u}")[:]
+            nc.vector.tensor_copy(b[u], source[u][:].indirect(second_list[u][:]))
+
+        def differ_on_vector(u, first):
+            d[u] = scratch(f"d{u}")
+            nc.vector.tensor_tensor(d[u][:], first, b[u], ALU.subtract)
 
         def fetch(u):
-            src, dst, first, second = units[u]
-            if u < PACK:
-                project(u)
-            window = src[u % PACK]
-            pair = sb.tile([P, 2, V], F32, name=f"pair{u}", tag="root1" if u == 2 else f"pair{u}", align_bytes=64)
+            pair = placed.tile([P, 2, V], F32, name=f"pair{u}", offset=(u - 2) * PAIR_BYTES)
             a[u], b[u] = pair[:, 0, :], pair[:, 1, :]
-            if u == 0:
-                nc.scalar.activation(a[u], window[:].indirect(first[:]), ACT.Copy)
-                nc.vector.tensor_copy(b[u], window[:].indirect(second[:]))
-                nc.vector.tensor_tensor(d[u][:], a[u], b[u], ALU.subtract)
-            elif u == 1:
-                nc.vector.tensor_copy(b[u], window[:].indirect(second[:]))
-                nc.vector.tensor_tensor(d[u][:], window[:].indirect(first[:]), b[u], ALU.subtract)
-                nc.gpsimd.tensor_tensor(a[u], d[u][:], b[u], ALU.add)
-            else:
-                nc.scalar.activation(a[u], window[:].indirect(first[:]), ACT.Copy)
-                nc.scalar.activation(b[u], window[:].indirect(second[:]), ACT.Copy)
-                nc.gpsimd.tensor_tensor(d[u][:], a[u], b[u], ALU.subtract)
+            gather_on_scalar(a[u], u, first_list[u])
+            gather_on_scalar(b[u], u, second_list[u])
+
+        def differ(u):
+            d[u] = scratch(f"d{u}", d_tag(u))
+            nc.gpsimd.tensor_tensor(d[u][:], a[u], b[u], ALU.subtract)
 
         def weigh(u):
-            nc.scalar.activation(size[u][:], d[u][:], ACT.Abs)
-            nc.scalar.activation(root[u][:], size[u][:], ACT.Abs_reciprocal_sqrt, bias=1.0)
-            nc.scalar.activation(r[u][:], root[u][:], ACT.Square, scale=math.sqrt(0.75))
-
-        def correct(u):
-            engine = nc.vector if u == 0 else nc.gpsimd
-            c[u] = sb.tile([P, V], F32, name=f"c{u}", tag="y1" if u == 0 else f"c{u}", align_bytes=64)
-            engine.tensor_tensor(c[u][:], d[u][:], r[u][:], ALU.mult)
+            size = scratch(f"size{u}")
+            if u % 2 == 1 and u < LAST:
+                border = u * PAIR_BYTES
+                root = placed.tile([P, V], F32, name=f"root{u}", offset=border - SCRATCH_BYTES // 2)
+            else:
+                root = scratch(f"root{u}")
+            r[u] = scratch(f"r{u}")
+            nc.scalar.activation(size[:], d[u][:], ACT.Abs)
+            nc.scalar.activation(root[:], size[:], ACT.Abs_reciprocal_sqrt, bias=1.0)
+            nc.scalar.activation(r[u][:], root[:], ACT.Square, scale=math.sqrt(0.75))
 
         def put_second(u):
-            src, dst, first, second = units[u]
             engine = nc.vector if u == 0 else nc.gpsimd
+            c[u] = scratch(f"c{u}")
+            engine.tensor_tensor(c[u][:], d[u][:], r[u][:], ALU.mult)
             engine.tensor_tensor(b[u], b[u], c[u][:], ALU.add)
-            nc.vector.tensor_copy(dst[u % PACK][:].indirect(second[:]), b[u])
+            nc.vector.tensor_copy(target[u][:].indirect(second_list[u][:]), b[u])
 
         def put_first(u):
-            src, dst, first, second = units[u]
-            moved = sb.tile([P, V], F32, name=f"moved{u}", tag=f"d{u + 1}" if u % 2 == 0 else f"moved{u}")
+            moved = scratch(f"moved{u}", d_tag(u + 1) if u >= 2 and u % 2 == 0 else None)
             nc.gpsimd.tensor_tensor(moved[:], a[u], c[u][:], ALU.subtract)
-            nc.vector.tensor_copy(dst[u % PACK][:].indirect(first[:]), moved[:])
+            nc.vector.tensor_copy(target[u][:].indirect(first_list[u][:]), moved[:])
 
-        fetch(0)
+        project(0)
+        fetch_first(0, None)
+        fetch_second_on_vector(0)
+        differ_on_vector(0, a[0])
         weigh(0)
-        fetch(1)
+        project(1)
+        fetch_second_on_vector(1)
+        differ_on_vector(1, source[1][:].indirect(first_list[1][:]))
         weigh(1)
-        for u in range(0, len(units), 2):
-            for v in (u, u + 1):
-                correct(v)
+        project(2)
+        project(3)
+        put_second(0)
+        put_first(0)
+        put_second(1)
+        fetch(2)
+        differ(2)
+        fetch_first(1, "r1")
+        put_first(1)
+        fetch(3)
+        differ(3)
+        weigh(2)
+        weigh(3)
+        for u in range(2, UNITS, 2):
+            pair_now = (u, u + 1)
+            pair_next = [v + 2 for v in pair_now if v + 2 <= LAST]
+            for v in pair_now:
                 put_second(v)
-            for v in (u, u + 1):
-                if v + 2 <= last:
-                    fetch(v + 2)
-                    weigh(v + 2)
+            for v in pair_next:
+                fetch(v)
+            for v in pair_now:
+                if pair_next:
+                    differ(v + 2)
                 put_first(v)
+            for v in pair_next:
+                weigh(v)
 
-
-        w2w, w2s = deal(w1w_raw, w1s_raw, "w2", nc.gpsimd, "root5", f"c{last}")
-        gain = sb.tile([P, PACK], F32, name="gain", tag="xqs", align_bytes=64)
+        w2w, w2s = deal("w2", f"r{LAST}")
+        gain = sb.tile([P, PACK], F32, name="gain", tag="picked_scales", align_bytes=64)
         nc.sync.dma_start(gain[:], gn.rearrange("(p t) o -> p (t o)", t=PACK))
-        z = sb.tile([P, S, PACK], BF16, name="z", tag=f"root{last}", align_bytes=64)
+        z = sb.tile([P, S, PACK], BF16, name="z", tag=f"root{LAST}", align_bytes=64)
         for t in range(PACK - 1):
             nc.scalar.activation(z[:, :, t], h3[t][:], ACT.Copy, scale=gain[:, t : t + 1])
-        ow = sb.tile([P, S], U32, name="ow", align_bytes=64)
-        osc = sb.tile([P, S], U8, name="osc", align_bytes=64)
+        out_codes = sb.tile([P, S], U32, name="out_codes", align_bytes=64)
+        out_scales = sb.tile([P, S], U8, name="out_scales", align_bytes=64)
         out_rows = out_0.rearrange("(p t) n -> p t n", t=PACK)
         out_words = out_1[0].rearrange("p n t -> p (n t)").bitcast(I32)
-        for ch in range(S // CH):
-            cols = slice(ch * CH, (ch + 1) * CH)
+        chunks = [slice(start, start + CHUNK) for start in range(0, S, CHUNK)]
+        for cols in chunks:
             nc.scalar.activation(z[:, cols, PACK - 1], h3[PACK - 1][:, cols], ACT.Copy, scale=gain[:, PACK - 1 : PACK])
-        for ch in range(S // CH):
-            cols = slice(ch * CH, (ch + 1) * CH)
-            zw = sb.tile([P, CH], U32, name=f"zw{ch}", align_bytes=64)
-            zs = sb.tile([P, CH], U8, name=f"zs{ch}", align_bytes=64)
-            nc.vector.quantize_mx(zw[:].bitcast(FP8X4), zs[:], z[:, cols, :].rearrange("p c t -> p (c t)"))
-            res = sb.tile([P, PACK, CH], F32, name=f"res{ch}")
-            for pair in range(2):
-                bank = psum.tile([P, 2, CH], F32, name="bank")
-                for j in range(2):
-                    t = 2 * pair + j
-                    nc.tensor.matmul_mx(
-                        bank[:, j, :],
-                        lhsT=w2w[:, 2 * P * t : 2 * P * (t + 1)].bitcast(FP4X4),
-                        lhsT_scale=w2s[:, P * t : P * (t + 1)],
-                        rhs=zw[:].bitcast(FP8X4),
-                        rhs_scale=zs[:],
-                        start=True,
-                        stop=True,
-                    )
-                if ch == 0:
-                    nc.vector.tensor_copy(res[:, 2 * pair : 2 * pair + 2, :], bank[:])
-                else:
-                    nc.scalar.copy(res[:, 2 * pair : 2 * pair + 2, :], bank[:])
-            nc.sync.dma_start(out_rows[:, :, cols], res[:])
-            rb = sb.tile([P, CH, PACK], BF16, name=f"rb{ch}", align_bytes=64)
+        for i, cols in enumerate(chunks):
+            z_codes = sb.tile([P, CHUNK], U32, name=f"z_codes{i}", align_bytes=64)
+            z_scales = sb.tile([P, CHUNK], U8, name=f"z_scales{i}", align_bytes=64)
+            nc.vector.quantize_mx(z_codes[:].bitcast(FP8X4), z_scales[:], z[:, cols, :].rearrange("p j t -> p (j t)"))
+            result = sb.tile([P, PACK, CHUNK], F32, name=f"result{i}")
+            for t in range(0, PACK, 2):
+                bank = psum.tile([P, 2, CHUNK], F32, name="bank")
+                for e in range(2):
+                    product(bank[:, e, :], w2w, w2s, t + e, z_codes[:], z_scales[:])
+                nc.scalar.copy(result[:, t : t + 2, :], bank[:])
+            nc.sync.dma_start(out_rows[:, :, cols], result[:])
+            rounded = sb.tile([P, CHUNK, PACK], BF16, name=f"rounded{i}", align_bytes=64)
             nc.vector.tensor_copy(
-                rb[:].rearrange("p (c i) t -> p c t i", i=4), res[:].rearrange("p t (c i) -> p c t i", i=4)
+                rounded[:].rearrange("p (j e) t -> p j t e", e=LINE),
+                result[:].rearrange("p t (j e) -> p j t e", e=LINE),
             )
-            nc.vector.quantize_mx(ow[:, cols].bitcast(FP8X4), osc[:, cols], rb[:].rearrange("p c t -> p (c t)"))
-            nc.sync.dma_start(out_words[:, cols], ow[:, cols].bitcast(I32))
-        for q in range(4):
+            nc.vector.quantize_mx(
+                out_codes[:, cols].bitcast(FP8X4), out_scales[:, cols], rounded[:].rearrange("p j t -> p (j t)")
+            )
+            nc.sync.dma_start(out_words[:, cols], out_codes[:, cols].bitcast(I32))
+        for q in range(QUADRANTS):
             queue = nc.sync if q % 2 else nc.scalar
-            queue.dma_start(out_2[0, 4 * q : 4 * q + 4, :].bitcast(I32), osc[32 * q : 32 * q + 4, :].bitcast(I32))
+            queue.dma_start(
+                out_2[0, 4 * q : 4 * q + 4, :].bitcast(I32), out_scales[32 * q : 32 * q + 4, :].bitcast(I32)
+            )

import math
from contextlib import ExitStack

import concourse.mybir as mybir

K, T, S, V, N, H = 512, 2048, 512, 256, 512, 512
FLOPS = 2 * K * H * S + 2 * H * N * S

F32 = mybir.dt.float32
BF16 = mybir.dt.bfloat16
I32 = mybir.dt.int32
U32 = mybir.dt.uint32
U16 = mybir.dt.uint16
U8 = mybir.dt.uint8
FP8X4 = mybir.dt.float8_e4m3fn_x4
FP4X4 = mybir.dt.float4_e2m1fn_x4
ACT = mybir.ActivationFunctionType
ALU = mybir.AluOpType

P = 128
PACK = 4
QUADRANTS = 4
BANKS = 8
HALF = S // 2
CHUNK = 128
LINE = 4
UNITS = 2 * PACK
LAST = UNITS - 1
SCRATCH_BYTES = V * 4
PAIR_BYTES = 2 * SCRATCH_BYTES


def tile_picked_pbd2_none_po_kernel(
    tc, x_words, x_scales, w1_words, w1_scales, gn, w2_words, w2_scales, offs, la, lb, ma, mb, out_0, out_1, out_2
):
    nc = tc.nc
    with ExitStack() as ctx:
        lists = ctx.enter_context(tc.tile_pool(name="lists", bufs=1))
        sb = ctx.enter_context(tc.tile_pool(name="sb", bufs=1))
        placed = ctx.enter_context(tc.tile_pool(name="placed", bufs=1))
        psum = ctx.enter_context(tc.psum_pool(name="psum", bufs=BANKS))

        def load_list(src, name):
            tile = lists.tile(list(src.shape), U16, name=name)
            nc.sync.dma_start(tile[:], src)
            return tile

        def load_scale_rows(queues, tile, src):
            for q in range(QUADRANTS):
                queues[q].dma_start(
                    tile[32 * q : 32 * q + 4, :].bitcast(I32), src[0, 4 * q : 4 * q + 4, :].bitcast(I32)
                )

        x_scale_table = sb.tile([P, T], U8, name="x_scale_table", align_bytes=64)
        w_scales_raw = sb.tile([P, H], U8, name="w_scales_raw", align_bytes=64)
        w_words_raw = sb.tile([P, 2 * H], U8, name="w_words_raw", align_bytes=64)
        x_word_table = sb.tile([P, T], U32, name="x_word_table", align_bytes=64)
        nc.vector.memset(x_scale_table[:].bitcast(I32), 0)
        nc.gpsimd.memset(w_scales_raw[:].bitcast(I32), 0)
        offs_t = load_list(offs, "offs_t")
        nc.sync.dma_start(w_words_raw[:].bitcast(I32), w1_words[0].bitcast(I32))
        la_t = load_list(la, "la_t")
        nc.sync.dma_start(x_word_table[:].bitcast(I32), x_words[0].rearrange("p n t -> p (n t)").bitcast(I32))
        load_scale_rows([nc.sync] * QUADRANTS, x_scale_table, x_scales)
        load_scale_rows([nc.sync, nc.sync, nc.gpsimd, nc.gpsimd], w_scales_raw, w1_scales)
        lb_t = load_list(lb, "lb_t")
        ma_t = load_list(ma, "ma_t")
        mb_t = load_list(mb, "mb_t")

        warm = sb.tile([P, 2], F32, name="warm")
        nc.vector.memset(warm[:, 0:1], 1.0)
        nc.scalar.activation(warm[:, 1:2], warm[:, 0:1], ACT.Abs_reciprocal_sqrt, bias=1.0)

        def deal(name, words_tag):
            words = sb.tile([P, 2 * H], U8, name=name + "_words", tag=words_tag, align_bytes=64)
            scales = sb.tile([P, H], U8, name=name + "_scales", tag="dealt_scales", align_bytes=64)
            nc.scalar.copy(
                words[:].bitcast(U16).rearrange("p (t m) -> p t m", t=PACK),
                w_words_raw[:].bitcast(U16).rearrange("p (m t) -> p t m", t=PACK),
            )
            nc.vector.tensor_copy(
                scales[:].rearrange("p (t m) -> p t m", t=PACK),
                w_scales_raw[:].rearrange("p (m t) -> p t m", t=PACK),
            )
            return words, scales

        def product(bank, words, scales, t, rhs_words, rhs_scales):
            nc.tensor.matmul_mx(
                bank,
                lhsT=words[:, 2 * P * t : 2 * P * (t + 1)].bitcast(FP4X4),
                lhsT_scale=scales[:, P * t : P * (t + 1)],
                rhs=rhs_words.bitcast(FP8X4),
                rhs_scale=rhs_scales,
                start=True,
                stop=True,
            )

        picked_scales = sb.tile([P, S], U8, name="picked_scales", align_bytes=64)
        nc.vector.tensor_copy(picked_scales[:], x_scale_table[:].indirect(offs_t[:]))
        w1w, w1s = deal("w1", "w1_words")
        nc.sync.dma_start(w_words_raw[:].bitcast(I32), w2_words[0].bitcast(I32))
        load_scale_rows([nc.sync] * QUADRANTS, w_scales_raw, w2_scales)
        picked_words = []
        for half in range(2):
            words = sb.tile([P, HALF], U32, name=f"picked_words{half}", align_bytes=64)
            entries = offs_t[:, half * HALF // 16 : (half + 1) * HALF // 16]
            nc.vector.tensor_copy(words[:], x_word_table[:].indirect(entries))
            picked_words.append(words)

        y = [sb.tile([P, S], F32, name=f"y{t}") for t in range(PACK)]

        def project(t):
            for half in range(2):
                cols = slice(half * HALF, (half + 1) * HALF)
                bank = psum.tile([P, HALF], F32, name="bank")
                product(bank[:], w1w, w1s, t, picked_words[half][:], picked_scales[:, cols])
                if t == 0 and half == 1:
                    nc.vector.tensor_copy(y[t][:, cols], bank[:])
                else:
                    nc.scalar.copy(y[t][:, cols], bank[:])

        h = [sb.tile([P, S], F32, name=f"h{t}") for t in range(PACK)]
        h3 = [sb.tile([P, S], F32, name=f"h3{t}") for t in range(PACK)]
        source, target = y + h, h + h3
        first_list = [la_t] * PACK + [ma_t] * PACK
        second_list = [lb_t] * PACK + [mb_t] * PACK
        a, b, d, r, c = {}, {}, {}, {}, {}

        def scratch(name, tag=None):
            return sb.tile([P, V], F32, name=name, tag=tag or name, align_bytes=64)

        def d_tag(u):
            if u < PACK:
                return f"d{u}"
            return f"r{u - 1}" if u % 2 == 0 else f"c{u - 3}"

        def gather_on_scalar(out, u, entries):
            nc.scalar.activation(out, source[u][:].indirect(entries[:]), ACT.Copy)

        def fetch_first(u, tag):
            a[u] = scratch(f"a{u}", tag)[:]
            gather_on_scalar(a[u], u, first_list[u])

        def fetch_second_on_vector(u):
            b[u] = scratch(f"b{u}")[:]
            nc.vector.tensor_copy(b[u], source[u][:].indirect(second_list[u][:]))

        def differ_on_vector(u, first):
            d[u] = scratch(f"d{u}")
            nc.vector.tensor_tensor(d[u][:], first, b[u], ALU.subtract)

        def fetch(u):
            pair = placed.tile([P, 2, V], F32, name=f"pair{u}", offset=(u - 2) * PAIR_BYTES)
            a[u], b[u] = pair[:, 0, :], pair[:, 1, :]
            gather_on_scalar(a[u], u, first_list[u])
            gather_on_scalar(b[u], u, second_list[u])

        def differ(u):
            d[u] = scratch(f"d{u}", d_tag(u))
            nc.gpsimd.tensor_tensor(d[u][:], a[u], b[u], ALU.subtract)

        def weigh(u):
            size = scratch(f"size{u}")
            if u % 2 == 1 and u < LAST:
                border = u * PAIR_BYTES
                root = placed.tile([P, V], F32, name=f"root{u}", offset=border - SCRATCH_BYTES // 2)
            else:
                root = scratch(f"root{u}")
            r[u] = scratch(f"r{u}")
            nc.scalar.activation(size[:], d[u][:], ACT.Abs)
            nc.scalar.activation(root[:], size[:], ACT.Abs_reciprocal_sqrt, bias=1.0)
            nc.scalar.activation(r[u][:], root[:], ACT.Square, scale=math.sqrt(0.75))

        def put_second(u):
            engine = nc.vector if u == 0 else nc.gpsimd
            c[u] = scratch(f"c{u}")
            engine.tensor_tensor(c[u][:], d[u][:], r[u][:], ALU.mult)
            engine.tensor_tensor(b[u], b[u], c[u][:], ALU.add)
            nc.vector.tensor_copy(target[u][:].indirect(second_list[u][:]), b[u])

        def put_first(u):
            moved = scratch(f"moved{u}", d_tag(u + 1) if u >= 2 and u % 2 == 0 else None)
            nc.gpsimd.tensor_tensor(moved[:], a[u], c[u][:], ALU.subtract)
            nc.vector.tensor_copy(target[u][:].indirect(first_list[u][:]), moved[:])

        project(0)
        fetch_first(0, None)
        fetch_second_on_vector(0)
        differ_on_vector(0, a[0])
        weigh(0)
        project(1)
        fetch_second_on_vector(1)
        differ_on_vector(1, source[1][:].indirect(first_list[1][:]))
        weigh(1)
        project(2)
        project(3)
        put_second(0)
        put_first(0)
        put_second(1)
        fetch(2)
        differ(2)
        fetch_first(1, "r1")
        put_first(1)
        fetch(3)
        differ(3)
        weigh(2)
        weigh(3)
        for u in range(2, UNITS, 2):
            pair_now = (u, u + 1)
            pair_next = [v + 2 for v in pair_now if v + 2 <= LAST]
            for v in pair_now:
                put_second(v)
            for v in pair_next:
                fetch(v)
            for v in pair_now:
                if pair_next:
                    differ(v + 2)
                put_first(v)
            for v in pair_next:
                weigh(v)

        w2w, w2s = deal("w2", f"r{LAST}")
        gain = sb.tile([P, PACK], F32, name="gain", tag="picked_scales", align_bytes=64)
        nc.sync.dma_start(gain[:], gn.rearrange("(p t) o -> p (t o)", t=PACK))
        z = sb.tile([P, S, PACK], BF16, name="z", tag=f"root{LAST}", align_bytes=64)
        for t in range(PACK - 1):
            nc.scalar.activation(z[:, :, t], h3[t][:], ACT.Copy, scale=gain[:, t : t + 1])
        out_codes = sb.tile([P, S], U32, name="out_codes", align_bytes=64)
        out_scales = sb.tile([P, S], U8, name="out_scales", align_bytes=64)
        out_rows = out_0.rearrange("(p t) n -> p t n", t=PACK)
        out_words = out_1[0].rearrange("p n t -> p (n t)").bitcast(I32)
        chunks = [slice(start, start + CHUNK) for start in range(0, S, CHUNK)]
        for cols in chunks:
            nc.scalar.activation(z[:, cols, PACK - 1], h3[PACK - 1][:, cols], ACT.Copy, scale=gain[:, PACK - 1 : PACK])
        for i, cols in enumerate(chunks):
            z_codes = sb.tile([P, CHUNK], U32, name=f"z_codes{i}", align_bytes=64)
            z_scales = sb.tile([P, CHUNK], U8, name=f"z_scales{i}", align_bytes=64)
            nc.vector.quantize_mx(z_codes[:].bitcast(FP8X4), z_scales[:], z[:, cols, :].rearrange("p j t -> p (j t)"))
            result = sb.tile([P, PACK, CHUNK], F32, name=f"result{i}")
            for t in range(0, PACK, 2):
                bank = psum.tile([P, 2, CHUNK], F32, name="bank")
                for e in range(2):
                    product(bank[:, e, :], w2w, w2s, t + e, z_codes[:], z_scales[:])
                nc.scalar.copy(result[:, t : t + 2, :], bank[:])
            nc.sync.dma_start(out_rows[:, :, cols], result[:])
            rounded = sb.tile([P, CHUNK, PACK], BF16, name=f"rounded{i}", align_bytes=64)
            nc.vector.tensor_copy(
                rounded[:].rearrange("p (j e) t -> p j t e", e=LINE),
                result[:].rearrange("p t (j e) -> p j t e", e=LINE),
            )
            nc.vector.quantize_mx(
                out_codes[:, cols].bitcast(FP8X4), out_scales[:, cols], rounded[:].rearrange("p j t -> p (j t)")
            )
            nc.sync.dma_start(out_words[:, cols], out_codes[:, cols].bitcast(I32))
        for q in range(QUADRANTS):
            queue = nc.sync if q % 2 else nc.scalar
            queue.dma_start(
                out_2[0, 4 * q : 4 * q + 4, :].bitcast(I32), out_scales[32 * q : 32 * q + 4, :].bitcast(I32)
            )
